import numpy as np
import ml_dtypes


def mxq(x, axis, fmt="e4m3"):
    dtype, down = {"e4m3": (ml_dtypes.float8_e4m3fn, 7), "e5m2": (ml_dtypes.float8_e5m2, 14)}[fmt]
    v = np.moveaxis(np.asarray(x, np.float32).astype(ml_dtypes.bfloat16).astype(np.float64), axis, -1)
    blocks = v.reshape(v.shape[:-1] + (-1, 32))
    amax = np.abs(blocks).max(-1, keepdims=True)
    byte = np.maximum(np.where(amax > 0, np.frexp(amax)[1] - 1 + 127, 0) - down, 1)
    scale = np.exp2(byte - 127.0)
    codes = (blocks / scale).astype(np.float32).astype(dtype).astype(np.float64)
    return np.moveaxis((codes * scale).reshape(v.shape), -1, axis)


WIDE = False


def mx_kscale(k):
    if not WIDE:
        return np.ones(k)
    levels = np.array([10, -10, 5, -5, 0])
    if k % 512:
        return np.exp2(np.random.permutation(np.resize(levels, k // 32))).repeat(32)
    a = np.empty((k // 512, 16))
    for p in range(k // 512):
        a[p, :8] = np.random.permutation(np.resize(levels, 8))
        for g in range(8):
            far = levels[np.abs(levels - a[p, g]) >= 10]
            a[p, g + 8] = far[np.random.randint(len(far))]
    return np.exp2(a.ravel()).repeat(32)


BF16 = ml_dtypes.bfloat16


def bf(x):
    return np.asarray(x, np.float32).astype(BF16)


def f64(x):
    return np.asarray(x).astype(np.float64)


B, D, H, N, T = 1024, 1024, 512, 1024, 3


def sigmoid(v):
    return 1.0 / (1.0 + np.exp(-v))


def draw0():
    s, t = mx_kscale(D), mx_kscale(H)
    return {"x": bf(np.random.standard_normal((B, D)) * s),
            "w": bf(np.random.standard_normal((D, H)) / np.sqrt(D) / s[:, None]),
            "g": bf((1.0 + 0.1 * np.random.standard_normal(H)) * t),
            "wh": bf(np.random.standard_normal((T, H, N)) * 1.5 / np.sqrt(H) / t[None, :, None]),
            "o": bf(np.random.uniform(0.0, 1.0, (B, N))),
            "y": bf(np.random.uniform(0.0, 1.0, (B, N)))}


def shared_trunk(x, w, g):
    return f64(g)[None, :] * np.tanh(mxq(f64(x), 1, "e4m3") @ mxq(f64(w), 0, "e4m3"))


def core(x, w, g, wh, o, y):
    h = shared_trunk(x, w, g)
    z = mxq(h, 1, "e4m3") @ mxq(f64(wh), 1, "e4m3")
    p = np.maximum(sigmoid(z[0]), 0.2)
    err = np.square(f64(y) - sigmoid(z[1]))
    e = z[2]
    return e + f64(o) * (err - e) / p


def e4m3fn_bytes(y):
    return np.clip(np.asarray(y, np.float64), -448.0, 448.0).astype(np.float32).astype(ml_dtypes.float8_e4m3fn).view(np.uint8)


def e4m3fn_values(b):
    return np.asarray(b, np.uint8).view(ml_dtypes.float8_e4m3fn).astype(np.float64)


def setup_inputs():
    d = draw0()
    x0 = np.asarray(d['wh']).astype(np.float64)
    s = (np.max(np.abs(x0), axis=(0, 2), keepdims=True) / 448.0).astype(np.float32)
    out = {}
    for k, v in d.items():
        if k == 'wh':
            out['wh_bytes'] = e4m3fn_bytes(x0 / s.astype(np.float64))
            out['wh_scale'] = s
        else:
            out[k] = v
    return out


def reference(x, w, g, wh_bytes, wh_scale, o, y):
    return core(x, w, g, e4m3fn_values(wh_bytes) * wh_scale.astype(np.float64), o, y)

@@ -1,0 +1,363 @@
+from contextlib import ExitStack
+
+import concourse.mybir as mybir
+from concourse.masks import make_identity
+
+B, D, H, N, T = 1024, 1024, 512, 1024, 3
+FLOPS = 2 * B * D * H + 2 * T * B * H * N
+
+F32 = mybir.dt.float32
+BF16 = mybir.dt.bfloat16
+U32 = mybir.dt.uint32
+U8 = mybir.dt.uint8
+FP8X4 = mybir.dt.float8_e4m3fn_x4
+FP8 = mybir.dt.float8_e4m3fn
+ACT = mybir.ActivationFunctionType
+ALU = mybir.AluOpType
+
+P = 128
+NT = 512
+NB = B // P
+NH = N // NT
+
+U_PE = set(range(4, 16))
+CLAMP_S = set(range(8))
+W_G = set([])
+MANUAL = False
+
+
+def tile_escmdoublyrobusterrormap_kernel(tc, x, w, g, wh_bytes, wh_scale, o, y, out):
+    nc = tc.nc
+    with ExitStack() as ctx:
+        const = ctx.enter_context(tc.tile_pool(name="const", bufs=1))
+        work = ctx.enter_context(tc.tile_pool(name="work", bufs=3))
+        psum = ctx.enter_context(tc.psum_pool(name="psum", bufs=1))
+        if MANUAL:
+            ctx.enter_context(tc.manual_schedule())
+
+        warm = const.tile([P, 1], F32)
+        nc.vector.memset(warm[:], 0.0)
+        nc.scalar.activation(out=warm[:], in_=warm[:], func=ACT.Exp)
+
+        s_sb = const.tile([P, 4], F32)
+        nc.scalar.dma_start(out=s_sb[:], in_=wh_scale.rearrange("o (p t) q -> p (o t q)", t=4))
+        g_bf = const.tile([P, 4], BF16)
+        nc.scalar.dma_start(out=g_bf[:], in_=g.rearrange("(p t) -> p t", t=4))
+
+        w_raw = {}
+        wh_b = {}
+        x_sb = {}
+        o_sb = {}
+        y_sb = {}
+
+        def load_w(c):
+            w_raw[c] = const.tile([P, 4, H], BF16, name="w_raw%d" % c)
+            nc.sync.dma_start(out=w_raw[c][:], in_=w[512 * c:512 * (c + 1), :].rearrange("(p j) c -> p j c", j=4))
+
+        def load_wh(t):
+            wh_b[t] = const.tile([P, 4, N], U8, name="wh_b%d" % t)
+            nc.sync.dma_start(out=wh_b[t][:], in_=wh_bytes[t].rearrange("(p j) n -> p j n", j=4))
+
+        def load_x(q):
+            x_sb[q] = const.tile([P, 2, D], BF16, name="x_sb%d" % q)
+            nc.sync.dma_start(out=x_sb[q][:], in_=x[256 * q:256 * (q + 1), :].rearrange("(i p) k -> p i k", p=P))
+
+        def load_oy(d, src, label, h, q):
+            d[h, q] = const.tile([P, 4, NT], BF16, name="%s_%d_%d" % (label, h, q))
+            nc.sync.dma_start(out=d[h, q][:], in_=src[512 * q:512 * (q + 1), NT * h:NT * (h + 1)].rearrange("(i p) n -> p i n", p=P))
+
+        load_w(0)
+        load_wh(1)
+        load_w(1)
+        load_wh(0)
+        load_x(0)
+        load_wh(2)
+        load_x(1)
+        load_oy(y_sb, y, "y", 0, 0)
+        load_oy(o_sb, o, "o", 0, 0)
+        load_x(2)
+        load_x(3)
+        load_oy(y_sb, y, "y", 0, 1)
+        load_oy(o_sb, o, "o", 0, 1)
+        load_oy(y_sb, y, "y", 1, 0)
+        load_oy(o_sb, o, "o", 1, 0)
+        load_oy(y_sb, y, "y", 1, 1)
+        load_oy(o_sb, o, "o", 1, 1)
+
+        ident = const.tile([P, P], F32)
+        make_identity(nc, ident[:])
+        neg2 = const.tile([P, P], BF16)
+        if U_PE:
+            nc.gpsimd.tensor_scalar(out=neg2[:], in0=ident[:], scalar1=-2.0, scalar2=0.0, op0=ALU.mult, op1=ALU.add)
+        g_sb = const.tile([P, 4], F32)
+        nc.gpsimd.tensor_copy(out=g_sb[:], in_=g_bf[:])
+
+        w_g = {}
+        w_q = const.tile([P, 2, H], U32, align_bytes=64)
+        w_s = const.tile([P, 2, H], U8, align_bytes=64)
+        x_g = {}
+        x_q = const.tile([P, NB, 2, P], U32, align_bytes=64)
+        x_s = const.tile([P, NB, 2, P], U8, align_bytes=64)
+        wh_p = {}
+        wh_g = {}
+        wh_q = const.tile([P, T, N], U32, align_bytes=64)
+        wh_s = const.tile([P, T, N], U8, align_bytes=64)
+        h_q = const.tile([P, NB, P], U32, align_bytes=64)
+        h_s = const.tile([P, NB, P], U8, align_bytes=64)
+        xt = {}
+        ht = {}
+        th = {}
+        hg = {}
+
+        def w_inter(c):
+            w_g[c] = const.tile([P, 4 * H], BF16, name="w_g%d" % c, align_bytes=64)
+            nc.vector.tensor_copy(
+                out=w_g[c][:].rearrange("p (t m j) -> p t m j", t=4, j=4),
+                in_=w_raw[c][:].rearrange("p j (m t) -> p t m j", t=4),
+            )
+
+        def w_quant(c):
+            nc.vector.quantize_mx(out=w_q[:, c, :].bitcast(FP8X4), scales=w_s[:, c, :], in_=w_g[c][:])
+
+        def x_trans(i):
+            xt[i] = psum.tile([P, 2, 2, P], F32, name="xt")
+            words = x_sb[i // 2][:, i % 2, :].bitcast(F32)
+            for c in range(2):
+                for u in range(2):
+                    nc.tensor.transpose(xt[i][:, c, u, :], words[:, 256 * c + u:256 * (c + 1):2], ident[:])
+
+        def x_copy(i):
+            x_g[i] = work.tile([P, 2 * P * 4], BF16, name="x_g", align_bytes=64)
+            nc.scalar.copy(
+                out=x_g[i][:].bitcast(F32).rearrange("p (c r u) -> p c r u", c=2, u=2),
+                in_=xt[i][:].rearrange("p c u r -> p c r u"),
+            )
+
+        def x_quant(i):
+            nc.vector.quantize_mx(
+                out=x_q[:, i, :, :].rearrange("p c r -> p (c r)").bitcast(FP8X4),
+                scales=x_s[:, i, :, :].rearrange("p c r -> p (c r)"),
+                in_=x_g[i][:],
+            )
+
+        def h_matmul(i):
+            ht[i] = psum.tile([P, 4, P], F32, name="ht")
+            for t in range(4):
+                for c in range(2):
+                    nc.tensor.matmul_mx(
+                        out=ht[i][:, t, :],
+                        lhsT=w_q[:, c, P * t:P * (t + 1)].bitcast(FP8X4),
+                        lhsT_scale=w_s[:, c, P * t:P * (t + 1)],
+                        rhs=x_q[:, i, c, :].bitcast(FP8X4),
+                        rhs_scale=x_s[:, i, c, :],
+                        start=(c == 0),
+                        stop=(c == 1),
+                    )
+
+        def h_tanh(i):
+            th[i] = work.tile([P, P, 4], F32, name="th")
+            nc.scalar.activation(out=th[i][:], in_=ht[i][:].rearrange("p t n -> p n t"), func=ACT.Tanh)
+
+        def h_gain(i):
+            hg[i] = work.tile([P, P, 4], BF16, name="hg", align_bytes=64)
+            nc.vector.tensor_tensor(out=hg[i][:], in0=th[i][:], in1=g_sb[:].unsqueeze(1).to_broadcast([P, P, 4]), op=ALU.mult)
+
+        def h_quant(i):
+            nc.vector.quantize_mx(
+                out=h_q[:, i, :].bitcast(FP8X4), scales=h_s[:, i, :], in_=hg[i][:].rearrange("p n t -> p (n t)")
+            )
+
+        def wh_widen(t, h, j):
+            if j == 0:
+                wh_p[t, h] = work.tile([P, 4, NT], BF16, name="wh_p")
+            nc.scalar.activation(
+                out=wh_p[t, h][:, j, :],
+                in_=wh_b[t][:, j, NT * h:NT * (h + 1)].bitcast(FP8),
+                func=ACT.Copy,
+                scale=s_sb[:, j:j + 1],
+            )
+
+        def wh_inter(t, h):
+            wh_g[t, h] = work.tile([P, NT, 4], BF16, name="wh_g", align_bytes=64)
+            nc.vector.tensor_copy(out=wh_g[t, h][:], in_=wh_p[t, h][:].rearrange("p j n -> p n j"))
+
+        def wh_quant(t, h):
+            nc.vector.quantize_mx(
+                out=wh_q[:, t, NT * h:NT * (h + 1)].bitcast(FP8X4),
+                scales=wh_s[:, t, NT * h:NT * (h + 1)],
+                in_=wh_g[t, h][:].rearrange("p n j -> p (n j)"),
+            )
+
+        z = {}
+        tt = {}
+        ee = {}
+        uu = {}
+        er = {}
+        ww = {}
+        ff = {}
+
+        def hi(s):
+            return s // NB, s % NB
+
+        def z_matmul(s, t):
+            h, i = hi(s)
+            if t == 1:
+                z1 = psum.tile([P, NT], F32, name="z1")
+                z[s, t] = z1
+            elif t == 0:
+                z0 = psum.tile([P, NT], F32, name="z0")
+                z[s, t] = z0
+            else:
+                z2 = psum.tile([P, NT], F32, name="z2", bufs=3)
+                z[s, t] = z2
+            nc.tensor.matmul_mx(
+                out=z[s, t][:],
+                lhsT=h_q[:, i, :].bitcast(FP8X4),
+                lhsT_scale=h_s[:, i, :],
+                rhs=wh_q[:, t, NT * h:NT * (h + 1)].bitcast(FP8X4),
+                rhs_scale=wh_s[:, t, NT * h:NT * (h + 1)],
+                start=True,
+                stop=True,
+            )
+
+        def b_tanh(s):
+            tt[s] = work.tile([P, NT], F32, name="tt")
+            nc.scalar.activation(out=tt[s][:], in_=z[s, 1][:], func=ACT.Tanh, scale=0.5)
+
+        def b_exp(s):
+            ee[s] = work.tile([P, NT], F32, name="ee")
+            nc.scalar.activation(out=ee[s][:], in_=z[s, 0][:], func=ACT.Exp, scale=-1.0)
+
+        def b_u(s):
+            h, i = hi(s)
+            ysl = y_sb[h, i // 4][:, i % 4, :]
+            if s in U_PE:
+                uu[s] = psum.tile([P, NT], F32, name="up")
+                nc.tensor.matmul(out=uu[s][:], lhsT=neg2[:], rhs=ysl, start=True, stop=False)
+                nc.tensor.matmul(out=uu[s][:], lhsT=ident[:], rhs=tt[s][:], start=False, stop=True)
+            else:
+                uu[s] = work.tile([P, NT], F32, name="us")
+                nc.vector.scalar_tensor_tensor(out=uu[s][:], in0=ysl, scalar=-2.0, in1=tt[s][:], op0=ALU.mult, op1=ALU.add)
+
+        def b_sq(s):
+            er[s] = work.tile([P, NT], F32, name="er")
+            nc.scalar.activation(out=er[s][:], in_=uu[s][:], func=ACT.Square, scale=0.5, bias=0.5)
+
+        def b_clamp(s):
+            if s in CLAMP_S:
+                nc.scalar.activation(out=ee[s][:], in_=ee[s][:], func=ACT.Relu, scale=-1.0, bias=4.0)
+            else:
+                nc.vector.tensor_scalar(out=ee[s][:], in0=ee[s][:], scalar1=4.0, scalar2=1.0, op0=ALU.min, op1=ALU.add)
+
+        def b_w(s):
+            h, i = hi(s)
+            osl = o_sb[h, i // 4][:, i % 4, :]
+            ww[s] = work.tile([P, NT], F32, name="ww")
+            if s in CLAMP_S:
+                nc.vector.scalar_tensor_tensor(out=ww[s][:], in0=ee[s][:], scalar=5.0, in1=osl, op0=ALU.subtract, op1=ALU.mult)
+            elif s in W_G:
+                nc.gpsimd.tensor_tensor(out=ww[s][:], in0=ee[s][:], in1=osl, op=ALU.mult)
+            else:
+                nc.vector.tensor_tensor(out=ww[s][:], in0=ee[s][:], in1=osl, op=ALU.mult)
+
+        def b_f(s):
+            ff[s] = work.tile([P, NT], F32, name="ff")
+            if s in CLAMP_S:
+                nc.vector.tensor_tensor(out=ff[s][:], in0=z[s, 2][:], in1=er[s][:], op=ALU.subtract)
+            else:
+                nc.vector.tensor_tensor(out=ff[s][:], in0=er[s][:], in1=z[s, 2][:], op=ALU.subtract)
+
+        def b_wf(s):
+            nc.vector.tensor_tensor(out=ff[s][:], in0=ww[s][:], in1=ff[s][:], op=ALU.mult)
+
+        def b_out(s):
+            h, i = hi(s)
+            ot = work.tile([P, NT], F32, name="ot")
+            nc.vector.tensor_tensor(out=ot[:], in0=z[s, 2][:], in1=ff[s][:], op=ALU.add)
+            nc.sync.dma_start(out=out[P * i:P * (i + 1), NT * h:NT * (h + 1)], in_=ot[:])
+
+        w_inter(0)
+        for j in range(4):
+            wh_widen(1, 0, j)
+        w_inter(1)
+        w_quant(0)
+        for j in range(4):
+            wh_widen(0, 0, j)
+        x_trans(0)
+        x_copy(0)
+        x_trans(1)
+        x_copy(1)
+        wh_inter(1, 0)
+        w_quant(1)
+        wh_quant(1, 0)
+        x_quant(0)
+        h_matmul(0)
+        wh_inter(0, 0)
+        x_quant(1)
+        for j in range(2):
+            wh_widen(2, 0, j)
+        h_tanh(0)
+        for j in range(2, 4):
+            wh_widen(2, 0, j)
+        h_matmul(1)
+        h_tanh(1)
+        x_trans(2)
+        x_copy(2)
+        x_trans(3)
+        x_copy(3)
+        wh_quant(0, 0)
+        h_gain(0)
+        wh_inter(2, 0)
+        h_quant(0)
+        wh_quant(2, 0)
+        x_quant(2)
+
+        later = [(t, 1, j) for t in (1, 0, 2) for j in range(4)]
+
+        S = NB * NH
+        for s in range(S + 2):
+            if s < S:
+                for t in (1, 0, 2):
+                    z_matmul(s, t)
+            if s + 4 < NB:
+                x_trans(s + 4)
+            if s + 2 < NB:
+                h_matmul(s + 2)
+            if s < S:
+                b_tanh(s)
+            if 1 <= s <= S:
+                b_sq(s - 1)
+                if s - 1 in CLAMP_S:
+                    b_clamp(s - 1)
+            if s < S:
+                b_exp(s)
+            if s + 2 < NB:
+                h_tanh(s + 2)
+            if s + 4 < NB:
+                x_copy(s + 4)
+            for k in later[2 * s:2 * s + 2]:
+                wh_widen(*k)
+            if 1 <= s <= S:
+                b_f(s - 1)
+                if s - 1 in CLAMP_S:
+                    b_w(s - 1)
+            if s < S:
+                b_u(s)
+            if s + 1 < NB:
+                h_gain(s + 1)
+            if s + 3 < NB and s >= 0:
+                x_quant(s + 3)
+            if s in (2, 4, 6):
+                wh_inter((1, 0, 2)[s // 2 - 1], 1)
+            if 1 <= s <= S:
+                b_wf(s - 1)
+            if s + 1 < NB:
+                h_quant(s + 1)
+            if s in (3, 5, 7):
+                wh_quant((1, 0, 2)[(s - 3) // 2], 1)
+            if s < S and s not in CLAMP_S:
+                b_clamp(s)
+            if 2 <= s:
+                b_out(s - 2)
+            if s < S and s not in CLAMP_S:
+                b_w(s)

@@ -16,14 +16,20 @@ ACT = mybir.ActivationFunctionType
 ALU = mybir.AluOpType
 
 P = 128
+BLOCKK = ('t', 'e', 'u', 'sq', 'r', 'f', 'w', 'wf', 'o', 'z0', 'z1', 'z2')
 NT = 512
 NB = B // P
 NH = N // NT
 
-U_PE = set(range(4, 16))
-CLAMP_S = set(range(8))
-W_G = set([])
-MANUAL = False
+U_PE = set(range(16))
+CLAMP_S = set([5,7,11])
+W_G = set([2,3,4,6,8,9,10,12,14,15])
+WIDEN_V = set([(0, 0, 0), (0, 0, 2), (0, 0, 3), (0, 1, 3), (1, 0, 1), (1, 0, 2), (1, 1, 0), (1, 1, 1), (1, 1, 3), (2, 0, 1), (2, 0, 3), (2, 1, 0)])
+IL_S = set([(0, 1), (1, 0)])
+G_GAIN = []
+IL_PE = set([])
+GSPLIT = 1
+CLAMP_G = set([1,2,3,4,6,8,9,10,11,12,13,14])
 
 
 def tile_escmdoublyrobusterrormap_kernel(tc, x, w, g, wh_bytes, wh_scale, o, y, out):
@@ -32,8 +38,7 @@ def tile_escmdoublyrobusterrormap_kernel(tc, x, w, g, wh_bytes, wh_scale, o, y, 
         const = ctx.enter_context(tc.tile_pool(name="const", bufs=1))
         work = ctx.enter_context(tc.tile_pool(name="work", bufs=3))
         psum = ctx.enter_context(tc.psum_pool(name="psum", bufs=1))
-        if MANUAL:
-            ctx.enter_context(tc.manual_schedule())
+        ctx.enter_context(tc.manual_schedule())
 
         warm = const.tile([P, 1], F32)
         nc.vector.memset(warm[:], 0.0)
@@ -54,35 +59,40 @@ def tile_escmdoublyrobusterrormap_kernel(tc, x, w, g, wh_bytes, wh_scale, o, y, 
             w_raw[c] = const.tile([P, 4, H], BF16, name="w_raw%d" % c)
             nc.sync.dma_start(out=w_raw[c][:], in_=w[512 * c:512 * (c + 1), :].rearrange("(p j) c -> p j c", j=4))
 
-        def load_wh(t):
-            wh_b[t] = const.tile([P, 4, N], U8, name="wh_b%d" % t)
-            nc.sync.dma_start(out=wh_b[t][:], in_=wh_bytes[t].rearrange("(p j) n -> p j n", j=4))
+        def load_wh(t, h):
+            if t not in wh_b:
+                wh_b[t] = const.tile([P, 4, N], U8, name="wh_b%d" % t)
+            c = slice(NT * h, NT * (h + 1))
+            nc.sync.dma_start(out=wh_b[t][:, :, c], in_=wh_bytes[t, :, c].rearrange("(p j) n -> p j n", j=4))
 
         def load_x(q):
             x_sb[q] = const.tile([P, 2, D], BF16, name="x_sb%d" % q)
             nc.sync.dma_start(out=x_sb[q][:], in_=x[256 * q:256 * (q + 1), :].rearrange("(i p) k -> p i k", p=P))
 
-        def load_oy(d, src, label, h, q):
-            d[h, q] = const.tile([P, 4, NT], BF16, name="%s_%d_%d" % (label, h, q))
-            nc.sync.dma_start(out=d[h, q][:], in_=src[512 * q:512 * (q + 1), NT * h:NT * (h + 1)].rearrange("(i p) n -> p i n", p=P))
+        def load_oy(d, src, label, q):
+            d[q] = const.tile([P, 2, N], BF16, name="%s_%d" % (label, q))
+            nc.sync.dma_start(out=d[q][:], in_=src[256 * q:256 * (q + 1), :].rearrange("(i p) n -> p i n", p=P))
 
+        load_wh(1, 0)
+        load_wh(0, 0)
         load_w(0)
-        load_wh(1)
-        load_w(1)
-        load_wh(0)
         load_x(0)
-        load_wh(2)
-        load_x(1)
-        load_oy(y_sb, y, "y", 0, 0)
-        load_oy(o_sb, o, "o", 0, 0)
+        load_wh(1, 1)
+        load_wh(0, 1)
+        load_w(1)
+        load_wh(2, 1)
+        load_wh(2, 0)
         load_x(2)
+        load_oy(o_sb, o, "o", 0)
+        load_oy(y_sb, y, "y", 0)
+        load_x(1)
         load_x(3)
-        load_oy(y_sb, y, "y", 0, 1)
-        load_oy(o_sb, o, "o", 0, 1)
-        load_oy(y_sb, y, "y", 1, 0)
-        load_oy(o_sb, o, "o", 1, 0)
-        load_oy(y_sb, y, "y", 1, 1)
-        load_oy(o_sb, o, "o", 1, 1)
+        load_oy(y_sb, y, "y", 1)
+        load_oy(o_sb, o, "o", 1)
+        load_oy(y_sb, y, "y", 2)
+        load_oy(o_sb, o, "o", 2)
+        load_oy(y_sb, y, "y", 3)
+        load_oy(o_sb, o, "o", 3)
 
         ident = const.tile([P, P], F32)
         make_identity(nc, ident[:])
@@ -120,7 +130,7 @@ def tile_escmdoublyrobusterrormap_kernel(tc, x, w, g, wh_bytes, wh_scale, o, y, 
             nc.vector.quantize_mx(out=w_q[:, c, :].bitcast(FP8X4), scales=w_s[:, c, :], in_=w_g[c][:])
 
         def x_trans(i):
-            xt[i] = psum.tile([P, 2, 2, P], F32, name="xt")
+            xt[i] = psum.tile([P, 2, 2, P], F32, name="xt", tag="aux", bufs=2)
             words = x_sb[i // 2][:, i % 2, :].bitcast(F32)
             for c in range(2):
                 for u in range(2):
@@ -141,7 +151,7 @@ def tile_escmdoublyrobusterrormap_kernel(tc, x, w, g, wh_bytes, wh_scale, o, y, 
             )
 
         def h_matmul(i):
-            ht[i] = psum.tile([P, 4, P], F32, name="ht")
+            ht[i] = psum.tile([P, 4, P], F32, name="ht", tag="aux", bufs=2)
             for t in range(4):
                 for c in range(2):
                     nc.tensor.matmul_mx(
@@ -168,18 +178,25 @@ def tile_escmdoublyrobusterrormap_kernel(tc, x, w, g, wh_bytes, wh_scale, o, y, 
             )
 
         def wh_widen(t, h, j):
-            if j == 0:
-                wh_p[t, h] = work.tile([P, 4, NT], BF16, name="wh_p")
-            nc.scalar.activation(
-                out=wh_p[t, h][:, j, :],
-                in_=wh_b[t][:, j, NT * h:NT * (h + 1)].bitcast(FP8),
-                func=ACT.Copy,
-                scale=s_sb[:, j:j + 1],
-            )
+            if (t, h) not in wh_p:
+                wh_p[t, h] = work.tile([P, 4, NT], BF16, name="wh_p", bufs=4)
+            if (t, h, j) in WIDEN_V:
+                nc.vector.tensor_scalar(
+                    out=wh_p[t, h][:, j, :], in0=wh_b[t][:, j, NT * h:NT * (h + 1)].bitcast(FP8), scalar1=s_sb[:, j:j + 1], scalar2=None, op0=ALU.mult)
+            else:
+                nc.scalar.activation(
+                    out=wh_p[t, h][:, j, :],
+                    in_=wh_b[t][:, j, NT * h:NT * (h + 1)].bitcast(FP8),
+                    func=ACT.Copy,
+                    scale=s_sb[:, j:j + 1],
+                )
 
         def wh_inter(t, h):
-            wh_g[t, h] = work.tile([P, NT, 4], BF16, name="wh_g", align_bytes=64)
-            nc.vector.tensor_copy(out=wh_g[t, h][:], in_=wh_p[t, h][:].rearrange("p j n -> p n j"))
+            wh_g[t, h] = work.tile([P, NT, 4], BF16, name="wh_g", align_bytes=64, bufs=4)
+            if (t, h) in IL_S:
+                nc.scalar.copy(out=wh_g[t, h][:], in_=wh_p[t, h][:].rearrange("p j n -> p n j"))
+            else:
+                nc.vector.tensor_copy(out=wh_g[t, h][:].rearrange("p (c i) j -> p c j i", i=4), in_=wh_p[t, h][:].rearrange("p j (c i) -> p c j i", i=4))
 
         def wh_quant(t, h):
             nc.vector.quantize_mx(
@@ -197,7 +214,7 @@ def tile_escmdoublyrobusterrormap_kernel(tc, x, w, g, wh_bytes, wh_scale, o, y, 
         ff = {}
 
         def hi(s):
-            return s // NB, s % NB
+            return s % 2, s // 2
 
         def z_matmul(s, t):
             h, i = hi(s)
@@ -210,6 +227,19 @@ def tile_escmdoublyrobusterrormap_kernel(tc, x, w, g, wh_bytes, wh_scale, o, y, 
             else:
                 z2 = psum.tile([P, NT], F32, name="z2", bufs=3)
                 z[s, t] = z2
+            if t == 1 and s in U_PE:
+                for c in range(4):
+                    cols = slice(NT * h + P * c, NT * h + P * (c + 1))
+                    nc.tensor.matmul_mx(
+                        out=z[s, t][:, P * c:P * (c + 1)],
+                        lhsT=wh_q[:, t, cols].bitcast(FP8X4),
+                        lhsT_scale=wh_s[:, t, cols],
+                        rhs=h_q[:, i, :].bitcast(FP8X4),
+                        rhs_scale=h_s[:, i, :],
+                        start=True,
+                        stop=True,
+                    )
+                return
             nc.tensor.matmul_mx(
                 out=z[s, t][:],
                 lhsT=h_q[:, i, :].bitcast(FP8X4),
@@ -225,38 +255,42 @@ def tile_escmdoublyrobusterrormap_kernel(tc, x, w, g, wh_bytes, wh_scale, o, y, 
             nc.scalar.activation(out=tt[s][:], in_=z[s, 1][:], func=ACT.Tanh, scale=0.5)
 
         def b_exp(s):
-            ee[s] = work.tile([P, NT], F32, name="ee")
+            ee[s] = work.tile([P, NT], F32, name="ee", bufs=4)
             nc.scalar.activation(out=ee[s][:], in_=z[s, 0][:], func=ACT.Exp, scale=-1.0)
 
         def b_u(s):
             h, i = hi(s)
-            ysl = y_sb[h, i // 4][:, i % 4, :]
+            ysl = y_sb[i // 2][:, i % 2, NT * h:NT * (h + 1)]
             if s in U_PE:
-                uu[s] = psum.tile([P, NT], F32, name="up")
+                uu[s] = psum.tile([P, NT], F32, name="up", bufs=1)
                 nc.tensor.matmul(out=uu[s][:], lhsT=neg2[:], rhs=ysl, start=True, stop=False)
-                nc.tensor.matmul(out=uu[s][:], lhsT=ident[:], rhs=tt[s][:], start=False, stop=True)
+                for c in range(4):
+                    cols = slice(P * c, P * (c + 1))
+                    nc.tensor.matmul(out=uu[s][:, cols], lhsT=tt[s][:, cols], rhs=ident[:], is_transpose=True, start=False, stop=(c == 3))
             else:
                 uu[s] = work.tile([P, NT], F32, name="us")
                 nc.vector.scalar_tensor_tensor(out=uu[s][:], in0=ysl, scalar=-2.0, in1=tt[s][:], op0=ALU.mult, op1=ALU.add)
 
         def b_sq(s):
-            er[s] = work.tile([P, NT], F32, name="er")
+            er[s] = work.tile([P, NT], F32, name="er", bufs=4)
             nc.scalar.activation(out=er[s][:], in_=uu[s][:], func=ACT.Square, scale=0.5, bias=0.5)
 
         def b_clamp(s):
             if s in CLAMP_S:
                 nc.scalar.activation(out=ee[s][:], in_=ee[s][:], func=ACT.Relu, scale=-1.0, bias=4.0)
             else:
-                nc.vector.tensor_scalar(out=ee[s][:], in0=ee[s][:], scalar1=4.0, scalar2=1.0, op0=ALU.min, op1=ALU.add)
+                (nc.gpsimd if s in CLAMP_G else nc.vector).tensor_scalar(out=ee[s][:], in0=ee[s][:], scalar1=4.0, scalar2=1.0, op0=ALU.min, op1=ALU.add)
 
         def b_w(s):
             h, i = hi(s)
-            osl = o_sb[h, i // 4][:, i % 4, :]
-            ww[s] = work.tile([P, NT], F32, name="ww")
+            osl = o_sb[i // 2][:, i % 2, NT * h:NT * (h + 1)]
+            ww[s] = work.tile([P, NT], F32, name="ww", bufs=4)
             if s in CLAMP_S:
                 nc.vector.scalar_tensor_tensor(out=ww[s][:], in0=ee[s][:], scalar=5.0, in1=osl, op0=ALU.subtract, op1=ALU.mult)
             elif s in W_G:
-                nc.gpsimd.tensor_tensor(out=ww[s][:], in0=ee[s][:], in1=osl, op=ALU.mult)
+                for q in range(GSPLIT):
+                    c = slice(NT // GSPLIT * q, NT // GSPLIT * (q + 1))
+                    nc.gpsimd.tensor_tensor(out=ww[s][:, c], in0=ee[s][:, c], in1=osl[:, c], op=ALU.mult)
             else:
                 nc.vector.tensor_tensor(out=ww[s][:], in0=ee[s][:], in1=osl, op=ALU.mult)
 
@@ -272,92 +306,25 @@ def tile_escmdoublyrobusterrormap_kernel(tc, x, w, g, wh_bytes, wh_scale, o, y, 
 
         def b_out(s):
             h, i = hi(s)
-            ot = work.tile([P, NT], F32, name="ot")
+            ot = work.tile([P, NT], F32, name="ot", bufs=4)
             nc.vector.tensor_tensor(out=ot[:], in0=z[s, 2][:], in1=ff[s][:], op=ALU.add)
             nc.sync.dma_start(out=out[P * i:P * (i + 1), NT * h:NT * (h + 1)], in_=ot[:])
 
-        w_inter(0)
-        for j in range(4):
-            wh_widen(1, 0, j)
-        w_inter(1)
-        w_quant(0)
-        for j in range(4):
-            wh_widen(0, 0, j)
-        x_trans(0)
-        x_copy(0)
-        x_trans(1)
-        x_copy(1)
-        wh_inter(1, 0)
-        w_quant(1)
-        wh_quant(1, 0)
-        x_quant(0)
-        h_matmul(0)
-        wh_inter(0, 0)
-        x_quant(1)
-        for j in range(2):
-            wh_widen(2, 0, j)
-        h_tanh(0)
-        for j in range(2, 4):
-            wh_widen(2, 0, j)
-        h_matmul(1)
-        h_tanh(1)
-        x_trans(2)
-        x_copy(2)
-        x_trans(3)
-        x_copy(3)
-        wh_quant(0, 0)
-        h_gain(0)
-        wh_inter(2, 0)
-        h_quant(0)
-        wh_quant(2, 0)
-        x_quant(2)
-
-        later = [(t, 1, j) for t in (1, 0, 2) for j in range(4)]
-
-        S = NB * NH
-        for s in range(S + 2):
-            if s < S:
-                for t in (1, 0, 2):
-                    z_matmul(s, t)
-            if s + 4 < NB:
-                x_trans(s + 4)
-            if s + 2 < NB:
-                h_matmul(s + 2)
-            if s < S:
-                b_tanh(s)
-            if 1 <= s <= S:
-                b_sq(s - 1)
-                if s - 1 in CLAMP_S:
-                    b_clamp(s - 1)
-            if s < S:
-                b_exp(s)
-            if s + 2 < NB:
-                h_tanh(s + 2)
-            if s + 4 < NB:
-                x_copy(s + 4)
-            for k in later[2 * s:2 * s + 2]:
-                wh_widen(*k)
-            if 1 <= s <= S:
-                b_f(s - 1)
-                if s - 1 in CLAMP_S:
-                    b_w(s - 1)
-            if s < S:
-                b_u(s)
-            if s + 1 < NB:
-                h_gain(s + 1)
-            if s + 3 < NB and s >= 0:
-                x_quant(s + 3)
-            if s in (2, 4, 6):
-                wh_inter((1, 0, 2)[s // 2 - 1], 1)
-            if 1 <= s <= S:
-                b_wf(s - 1)
-            if s + 1 < NB:
-                h_quant(s + 1)
-            if s in (3, 5, 7):
-                wh_quant((1, 0, 2)[(s - 3) // 2], 1)
-            if s < S and s not in CLAMP_S:
-                b_clamp(s)
-            if 2 <= s:
-                b_out(s - 2)
-            if s < S and s not in CLAMP_S:
-                b_w(s)
+        calls = {
+            "wid": wh_widen, "il": wh_inter, "q": wh_quant, "wil": w_inter, "wq": w_quant, "X": x_trans, "Xc": x_copy, "Xq": x_quant,
+            "H": h_matmul, "Ht": h_tanh, "G": h_gain, "Q": h_quant, "t": b_tanh, "e": b_exp, "u": b_u, "sq": b_sq,
+            "r": b_clamp, "f": b_f, "w": b_w, "wf": b_wf, "o": b_out,
+            "z0": lambda s: z_matmul(s, 0), "z1": lambda s: z_matmul(s, 1), "z2": lambda s: z_matmul(s, 2),
+        }
+        HEAD = [("wid", 1, 0, 3), ("X", 0), ("wid", 1, 0, 2), ("wid", 1, 0, 1), ("wid", 0, 0, 2), ("wid", 0, 0, 0), ("wid", 0, 0, 3), ("wil", 0), ("wid", 1, 0, 0), ("wid", 0, 0, 1), ("X", 1), ("il", 0, 0), ("wid", 1, 1, 1), ("wid", 1, 1, 3), ("il", 1, 0), ("wid", 1, 1, 0), ("wid", 1, 1, 2), ("wil", 1), ("wq", 0), ("Xc", 0), ("wq", 1), ("Xq", 0), ("wid", 0, 1, 2), ("Xc", 1), ("wid", 2, 1, 3), ("Xq", 1), ("wid", 2, 1, 0), ("H", 0), ("wid", 0, 1, 1), ("wid", 2, 0, 0), ("wid", 0, 1, 0), ("wid", 2, 1, 2), ("il", 1, 1), ("wid", 2, 0, 2), ("wid", 0, 1, 3), ("wid", 2, 1, 1), ("H", 1), ("wid", 2, 0, 3), ("Ht", 0), ("q", 0, 0), ("Ht", 1), ("X", 3), ("G", 0), ("il", 0, 1), ("wid", 2, 0, 1), ("il", 2, 1), ("X", 2), ("Q", 0), ("q", 1, 0), ("q", 1, 1), ("Xc", 3), ("q", 0, 1), ("il", 2, 0), ("z0", 0), ("Xc", 2), ("Xq", 2), ("Xq", 3), ("q", 2, 0), ("q", 2, 1), ("z1", 0)]
+        SLOT = [("X", 5, 0), ("z2", 0, 1), ("f", 0, 0), ("t", 1, 0), ("G", 2, 0), ("z1", 1, 1), ("w", 0, 0), ("w", 0, 1), ("e", 1, 0), ("Xc", 5, 0), ("f", 0, 1), ("t", 1, 1), ("Xq", 4, 0), ("z0", 1, 1), ("u", 1, 0), ("H", 3, 0), ("e", 1, 1), ("r", 1, 0), ("z2", 1, 0), ("Q", 2, 0), ("wf", 0, 0), ("sq", 1, 0), ("u", 1, 1), ("wf", 0, 1), ("z1", 2, 0), ("r", 1, 1), ("z0", 2, 0), ("Ht", 3, 0), ("o", 0, 0), ("o", 0, 1), ("sq", 1, 1)]
+        done = set()
+        for task in HEAD:
+            calls[task[0]](*task[1:])
+            done.add(task)
+        for i in range(-1, NB + 1):
+            for k, d, h in SLOT:
+                task = (k, 2 * (i + d) + h) if k in BLOCKK else (k, i + d)
+                if 0 <= i + d < NB and task not in done:
+                    calls[k](*task[1:])
+                    done.add(task)

@@ -22,14 +22,14 @@ NB = B // P
 NH = N // NT
 
 U_PE = set(range(16))
-CLAMP_S = set([5,7,11])
-W_G = set([2,3,4,6,8,9,10,12,14,15])
-WIDEN_V = set([(0, 0, 0), (0, 0, 2), (0, 0, 3), (0, 1, 3), (1, 0, 1), (1, 0, 2), (1, 1, 0), (1, 1, 1), (1, 1, 3), (2, 0, 1), (2, 0, 3), (2, 1, 0)])
+CLAMP_S = set([])
+W_G = set([0,1,2,3,4,5,6,7,8,9,10,11,12,13,14,15])
+WIDEN_V = set([(0, 0, 0), (0, 0, 1), (0, 0, 2), (0, 1, 0), (1, 0, 0), (1, 0, 1), (1, 1, 0), (1, 1, 1), (2, 0, 0), (2, 1, 0), (2, 1, 1)])
 IL_S = set([(0, 1), (1, 0)])
 G_GAIN = []
 IL_PE = set([])
 GSPLIT = 1
-CLAMP_G = set([1,2,3,4,6,8,9,10,11,12,13,14])
+CLAMP_G = set([])
 
 
 def tile_escmdoublyrobusterrormap_kernel(tc, x, w, g, wh_bytes, wh_scale, o, y, out):
@@ -77,16 +77,16 @@ def tile_escmdoublyrobusterrormap_kernel(tc, x, w, g, wh_bytes, wh_scale, o, y, 
         load_wh(0, 0)
         load_w(0)
         load_x(0)
-        load_wh(1, 1)
-        load_wh(0, 1)
         load_w(1)
         load_wh(2, 1)
         load_wh(2, 0)
-        load_x(2)
-        load_oy(o_sb, o, "o", 0)
+        load_wh(0, 1)
+        load_wh(1, 1)
         load_oy(y_sb, y, "y", 0)
-        load_x(1)
+        load_oy(o_sb, o, "o", 0)
+        load_x(2)
         load_x(3)
+        load_x(1)
         load_oy(y_sb, y, "y", 1)
         load_oy(o_sb, o, "o", 1)
         load_oy(y_sb, y, "y", 2)
@@ -316,8 +316,8 @@ def tile_escmdoublyrobusterrormap_kernel(tc, x, w, g, wh_bytes, wh_scale, o, y, 
             "r": b_clamp, "f": b_f, "w": b_w, "wf": b_wf, "o": b_out,
             "z0": lambda s: z_matmul(s, 0), "z1": lambda s: z_matmul(s, 1), "z2": lambda s: z_matmul(s, 2),
         }
-        HEAD = [("wid", 1, 0, 3), ("X", 0), ("wid", 1, 0, 2), ("wid", 1, 0, 1), ("wid", 0, 0, 2), ("wid", 0, 0, 0), ("wid", 0, 0, 3), ("wil", 0), ("wid", 1, 0, 0), ("wid", 0, 0, 1), ("X", 1), ("il", 0, 0), ("wid", 1, 1, 1), ("wid", 1, 1, 3), ("il", 1, 0), ("wid", 1, 1, 0), ("wid", 1, 1, 2), ("wil", 1), ("wq", 0), ("Xc", 0), ("wq", 1), ("Xq", 0), ("wid", 0, 1, 2), ("Xc", 1), ("wid", 2, 1, 3), ("Xq", 1), ("wid", 2, 1, 0), ("H", 0), ("wid", 0, 1, 1), ("wid", 2, 0, 0), ("wid", 0, 1, 0), ("wid", 2, 1, 2), ("il", 1, 1), ("wid", 2, 0, 2), ("wid", 0, 1, 3), ("wid", 2, 1, 1), ("H", 1), ("wid", 2, 0, 3), ("Ht", 0), ("q", 0, 0), ("Ht", 1), ("X", 3), ("G", 0), ("il", 0, 1), ("wid", 2, 0, 1), ("il", 2, 1), ("X", 2), ("Q", 0), ("q", 1, 0), ("q", 1, 1), ("Xc", 3), ("q", 0, 1), ("il", 2, 0), ("z0", 0), ("Xc", 2), ("Xq", 2), ("Xq", 3), ("q", 2, 0), ("q", 2, 1), ("z1", 0)]
-        SLOT = [("X", 5, 0), ("z2", 0, 1), ("f", 0, 0), ("t", 1, 0), ("G", 2, 0), ("z1", 1, 1), ("w", 0, 0), ("w", 0, 1), ("e", 1, 0), ("Xc", 5, 0), ("f", 0, 1), ("t", 1, 1), ("Xq", 4, 0), ("z0", 1, 1), ("u", 1, 0), ("H", 3, 0), ("e", 1, 1), ("r", 1, 0), ("z2", 1, 0), ("Q", 2, 0), ("wf", 0, 0), ("sq", 1, 0), ("u", 1, 1), ("wf", 0, 1), ("z1", 2, 0), ("r", 1, 1), ("z0", 2, 0), ("Ht", 3, 0), ("o", 0, 0), ("o", 0, 1), ("sq", 1, 1)]
+        HEAD = [("wid", 1, 0, 1), ("wid", 1, 0, 0), ("wid", 0, 0, 2), ("X", 1), ("X", 0), ("wid", 0, 0, 0), ("wid", 1, 0, 3), ("wid", 0, 0, 3), ("wid", 1, 0, 2), ("il", 1, 0), ("Xc", 1), ("wid", 0, 0, 1), ("wil", 0), ("Xc", 0), ("wid", 2, 0, 2), ("il", 0, 0), ("wil", 1), ("wid", 1, 1, 3), ("wq", 0), ("wid", 0, 1, 0), ("wq", 1), ("Xq", 1), ("wid", 1, 1, 0), ("Xq", 0), ("wid", 2, 0, 1), ("wid", 1, 1, 1), ("wid", 2, 0, 3), ("wid", 2, 1, 0), ("q", 0, 0), ("H", 1), ("wid", 0, 1, 2), ("wid", 2, 1, 2), ("H", 0), ("wid", 2, 1, 3), ("wid", 2, 1, 1), ("wid", 2, 0, 0), ("wid", 0, 1, 1), ("il", 2, 1), ("Ht", 0), ("wid", 1, 1, 2), ("wid", 0, 1, 3), ("Ht", 1), ("X", 3), ("X", 2), ("q", 1, 0), ("G", 0), ("il", 1, 1), ("Q", 0), ("il", 2, 0), ("q", 1, 1), ("q", 2, 0), ("q", 2, 1), ("il", 0, 1), ("z0", 0), ("Xc", 3), ("Xc", 2), ("z1", 0), ("q", 0, 1), ("Xq", 2), ("Xq", 3)]
+        SLOT = [("z2", 0, 1), ("Xq", 4, 0), ("G", 2, 0), ("w", 0, 0), ("w", 0, 1), ("t", 1, 0), ("f", 0, 0), ("f", 0, 1), ("e", 1, 0), ("X", 5, 0), ("z2", 1, 0), ("wf", 0, 0), ("z1", 1, 1), ("r", 1, 0), ("Xc", 5, 0), ("u", 1, 0), ("z0", 1, 1), ("Q", 2, 0), ("wf", 0, 1), ("t", 1, 1), ("H", 3, 0), ("sq", 1, 0), ("u", 1, 1), ("o", 0, 0), ("e", 1, 1), ("z1", 2, 0), ("Ht", 3, 0), ("o", 0, 1), ("sq", 1, 1), ("r", 1, 1), ("z0", 2, 0)]
         done = set()
         for task in HEAD:
             calls[task[0]](*task[1:])

from contextlib import ExitStack

import concourse.mybir as mybir
from concourse.masks import make_identity

B, D, H, N, T = 1024, 1024, 512, 1024, 3
FLOPS = 2 * B * D * H + 2 * T * B * H * N

F32 = mybir.dt.float32
BF16 = mybir.dt.bfloat16
U32 = mybir.dt.uint32
U8 = mybir.dt.uint8
FP8X4 = mybir.dt.float8_e4m3fn_x4
FP8 = mybir.dt.float8_e4m3fn
ACT = mybir.ActivationFunctionType
ALU = mybir.AluOpType

P = 128
BLOCKK = ('t', 'e', 'u', 'sq', 'r', 'f', 'w', 'wf', 'o', 'z0', 'z1', 'z2')
NT = 512
NB = B // P
NH = N // NT

U_PE = set(range(16))
CLAMP_S = set([])
W_G = set([0,1,2,3,4,5,6,7,8,9,10,11,12,13,14,15])
WIDEN_V = set([(0, 0, 0), (0, 0, 1), (0, 0, 2), (0, 1, 0), (1, 0, 0), (1, 0, 1), (1, 1, 0), (1, 1, 1), (2, 0, 0), (2, 1, 0), (2, 1, 1)])
IL_S = set([(0, 1), (1, 0)])
G_GAIN = []
IL_PE = set([])
GSPLIT = 1
CLAMP_G = set([])


def tile_escmdoublyrobusterrormap_kernel(tc, x, w, g, wh_bytes, wh_scale, o, y, out):
    nc = tc.nc
    with ExitStack() as ctx:
        const = ctx.enter_context(tc.tile_pool(name="const", bufs=1))
        work = ctx.enter_context(tc.tile_pool(name="work", bufs=3))
        psum = ctx.enter_context(tc.psum_pool(name="psum", bufs=1))
        ctx.enter_context(tc.manual_schedule())

        warm = const.tile([P, 1], F32)
        nc.vector.memset(warm[:], 0.0)
        nc.scalar.activation(out=warm[:], in_=warm[:], func=ACT.Exp)

        s_sb = const.tile([P, 4], F32)
        nc.scalar.dma_start(out=s_sb[:], in_=wh_scale.rearrange("o (p t) q -> p (o t q)", t=4))
        g_bf = const.tile([P, 4], BF16)
        nc.scalar.dma_start(out=g_bf[:], in_=g.rearrange("(p t) -> p t", t=4))

        w_raw = {}
        wh_b = {}
        x_sb = {}
        o_sb = {}
        y_sb = {}

        def load_w(c):
            w_raw[c] = const.tile([P, 4, H], BF16, name="w_raw%d" % c)
            nc.sync.dma_start(out=w_raw[c][:], in_=w[512 * c:512 * (c + 1), :].rearrange("(p j) c -> p j c", j=4))

        def load_wh(t, h):
            if t not in wh_b:
                wh_b[t] = const.tile([P, 4, N], U8, name="wh_b%d" % t)
            c = slice(NT * h, NT * (h + 1))
            nc.sync.dma_start(out=wh_b[t][:, :, c], in_=wh_bytes[t, :, c].rearrange("(p j) n -> p j n", j=4))

        def load_x(q):
            x_sb[q] = const.tile([P, 2, D], BF16, name="x_sb%d" % q)
            nc.sync.dma_start(out=x_sb[q][:], in_=x[256 * q:256 * (q + 1), :].rearrange("(i p) k -> p i k", p=P))

        def load_oy(d, src, label, q):
            d[q] = const.tile([P, 2, N], BF16, name="%s_%d" % (label, q))
            nc.sync.dma_start(out=d[q][:], in_=src[256 * q:256 * (q + 1), :].rearrange("(i p) n -> p i n", p=P))

        load_wh(1, 0)
        load_wh(0, 0)
        load_w(0)
        load_x(0)
        load_w(1)
        load_wh(2, 1)
        load_wh(2, 0)
        load_wh(0, 1)
        load_wh(1, 1)
        load_oy(y_sb, y, "y", 0)
        load_oy(o_sb, o, "o", 0)
        load_x(2)
        load_x(3)
        load_x(1)
        load_oy(y_sb, y, "y", 1)
        load_oy(o_sb, o, "o", 1)
        load_oy(y_sb, y, "y", 2)
        load_oy(o_sb, o, "o", 2)
        load_oy(y_sb, y, "y", 3)
        load_oy(o_sb, o, "o", 3)

        ident = const.tile([P, P], F32)
        make_identity(nc, ident[:])
        neg2 = const.tile([P, P], BF16)
        if U_PE:
            nc.gpsimd.tensor_scalar(out=neg2[:], in0=ident[:], scalar1=-2.0, scalar2=0.0, op0=ALU.mult, op1=ALU.add)
        g_sb = const.tile([P, 4], F32)
        nc.gpsimd.tensor_copy(out=g_sb[:], in_=g_bf[:])

        w_g = {}
        w_q = const.tile([P, 2, H], U32, align_bytes=64)
        w_s = const.tile([P, 2, H], U8, align_bytes=64)
        x_g = {}
        x_q = const.tile([P, NB, 2, P], U32, align_bytes=64)
        x_s = const.tile([P, NB, 2, P], U8, align_bytes=64)
        wh_p = {}
        wh_g = {}
        wh_q = const.tile([P, T, N], U32, align_bytes=64)
        wh_s = const.tile([P, T, N], U8, align_bytes=64)
        h_q = const.tile([P, NB, P], U32, align_bytes=64)
        h_s = const.tile([P, NB, P], U8, align_bytes=64)
        xt = {}
        ht = {}
        th = {}
        hg = {}

        def w_inter(c):
            w_g[c] = const.tile([P, 4 * H], BF16, name="w_g%d" % c, align_bytes=64)
            nc.vector.tensor_copy(
                out=w_g[c][:].rearrange("p (t m j) -> p t m j", t=4, j=4),
                in_=w_raw[c][:].rearrange("p j (m t) -> p t m j", t=4),
            )

        def w_quant(c):
            nc.vector.quantize_mx(out=w_q[:, c, :].bitcast(FP8X4), scales=w_s[:, c, :], in_=w_g[c][:])

        def x_trans(i):
            xt[i] = psum.tile([P, 2, 2, P], F32, name="xt", tag="aux", bufs=2)
            words = x_sb[i // 2][:, i % 2, :].bitcast(F32)
            for c in range(2):
                for u in range(2):
                    nc.tensor.transpose(xt[i][:, c, u, :], words[:, 256 * c + u:256 * (c + 1):2], ident[:])

        def x_copy(i):
            x_g[i] = work.tile([P, 2 * P * 4], BF16, name="x_g", align_bytes=64)
            nc.scalar.copy(
                out=x_g[i][:].bitcast(F32).rearrange("p (c r u) -> p c r u", c=2, u=2),
                in_=xt[i][:].rearrange("p c u r -> p c r u"),
            )

        def x_quant(i):
            nc.vector.quantize_mx(
                out=x_q[:, i, :, :].rearrange("p c r -> p (c r)").bitcast(FP8X4),
                scales=x_s[:, i, :, :].rearrange("p c r -> p (c r)"),
                in_=x_g[i][:],
            )

        def h_matmul(i):
            ht[i] = psum.tile([P, 4, P], F32, name="ht", tag="aux", bufs=2)
            for t in range(4):
                for c in range(2):
                    nc.tensor.matmul_mx(
                        out=ht[i][:, t, :],
                        lhsT=w_q[:, c, P * t:P * (t + 1)].bitcast(FP8X4),
                        lhsT_scale=w_s[:, c, P * t:P * (t + 1)],
                        rhs=x_q[:, i, c, :].bitcast(FP8X4),
                        rhs_scale=x_s[:, i, c, :],
                        start=(c == 0),
                        stop=(c == 1),
                    )

        def h_tanh(i):
            th[i] = work.tile([P, P, 4], F32, name="th")
            nc.scalar.activation(out=th[i][:], in_=ht[i][:].rearrange("p t n -> p n t"), func=ACT.Tanh)

        def h_gain(i):
            hg[i] = work.tile([P, P, 4], BF16, name="hg", align_bytes=64)
            nc.vector.tensor_tensor(out=hg[i][:], in0=th[i][:], in1=g_sb[:].unsqueeze(1).to_broadcast([P, P, 4]), op=ALU.mult)

        def h_quant(i):
            nc.vector.quantize_mx(
                out=h_q[:, i, :].bitcast(FP8X4), scales=h_s[:, i, :], in_=hg[i][:].rearrange("p n t -> p (n t)")
            )

        def wh_widen(t, h, j):
            if (t, h) not in wh_p:
                wh_p[t, h] = work.tile([P, 4, NT], BF16, name="wh_p", bufs=4)
            if (t, h, j) in WIDEN_V:
                nc.vector.tensor_scalar(
                    out=wh_p[t, h][:, j, :], in0=wh_b[t][:, j, NT * h:NT * (h + 1)].bitcast(FP8), scalar1=s_sb[:, j:j + 1], scalar2=None, op0=ALU.mult)
            else:
                nc.scalar.activation(
                    out=wh_p[t, h][:, j, :],
                    in_=wh_b[t][:, j, NT * h:NT * (h + 1)].bitcast(FP8),
                    func=ACT.Copy,
                    scale=s_sb[:, j:j + 1],
                )

        def wh_inter(t, h):
            wh_g[t, h] = work.tile([P, NT, 4], BF16, name="wh_g", align_bytes=64, bufs=4)
            if (t, h) in IL_S:
                nc.scalar.copy(out=wh_g[t, h][:], in_=wh_p[t, h][:].rearrange("p j n -> p n j"))
            else:
                nc.vector.tensor_copy(out=wh_g[t, h][:].rearrange("p (c i) j -> p c j i", i=4), in_=wh_p[t, h][:].rearrange("p j (c i) -> p c j i", i=4))

        def wh_quant(t, h):
            nc.vector.quantize_mx(
                out=wh_q[:, t, NT * h:NT * (h + 1)].bitcast(FP8X4),
                scales=wh_s[:, t, NT * h:NT * (h + 1)],
                in_=wh_g[t, h][:].rearrange("p n j -> p (n j)"),
            )

        z = {}
        tt = {}
        ee = {}
        uu = {}
        er = {}
        ww = {}
        ff = {}

        def hi(s):
            return s % 2, s // 2

        def z_matmul(s, t):
            h, i = hi(s)
            if t == 1:
                z1 = psum.tile([P, NT], F32, name="z1")
                z[s, t] = z1
            elif t == 0:
                z0 = psum.tile([P, NT], F32, name="z0")
                z[s, t] = z0
            else:
                z2 = psum.tile([P, NT], F32, name="z2", bufs=3)
                z[s, t] = z2
            if t == 1 and s in U_PE:
                for c in range(4):
                    cols = slice(NT * h + P * c, NT * h + P * (c + 1))
                    nc.tensor.matmul_mx(
                        out=z[s, t][:, P * c:P * (c + 1)],
                        lhsT=wh_q[:, t, cols].bitcast(FP8X4),
                        lhsT_scale=wh_s[:, t, cols],
                        rhs=h_q[:, i, :].bitcast(FP8X4),
                        rhs_scale=h_s[:, i, :],
                        start=True,
                        stop=True,
                    )
                return
            nc.tensor.matmul_mx(
                out=z[s, t][:],
                lhsT=h_q[:, i, :].bitcast(FP8X4),
                lhsT_scale=h_s[:, i, :],
                rhs=wh_q[:, t, NT * h:NT * (h + 1)].bitcast(FP8X4),
                rhs_scale=wh_s[:, t, NT * h:NT * (h + 1)],
                start=True,
                stop=True,
            )

        def b_tanh(s):
            tt[s] = work.tile([P, NT], F32, name="tt")
            nc.scalar.activation(out=tt[s][:], in_=z[s, 1][:], func=ACT.Tanh, scale=0.5)

        def b_exp(s):
            ee[s] = work.tile([P, NT], F32, name="ee", bufs=4)
            nc.scalar.activation(out=ee[s][:], in_=z[s, 0][:], func=ACT.Exp, scale=-1.0)

        def b_u(s):
            h, i = hi(s)
            ysl = y_sb[i // 2][:, i % 2, NT * h:NT * (h + 1)]
            if s in U_PE:
                uu[s] = psum.tile([P, NT], F32, name="up", bufs=1)
                nc.tensor.matmul(out=uu[s][:], lhsT=neg2[:], rhs=ysl, start=True, stop=False)
                for c in range(4):
                    cols = slice(P * c, P * (c + 1))
                    nc.tensor.matmul(out=uu[s][:, cols], lhsT=tt[s][:, cols], rhs=ident[:], is_transpose=True, start=False, stop=(c == 3))
            else:
                uu[s] = work.tile([P, NT], F32, name="us")
                nc.vector.scalar_tensor_tensor(out=uu[s][:], in0=ysl, scalar=-2.0, in1=tt[s][:], op0=ALU.mult, op1=ALU.add)

        def b_sq(s):
            er[s] = work.tile([P, NT], F32, name="er", bufs=4)
            nc.scalar.activation(out=er[s][:], in_=uu[s][:], func=ACT.Square, scale=0.5, bias=0.5)

        def b_clamp(s):
            if s in CLAMP_S:
                nc.scalar.activation(out=ee[s][:], in_=ee[s][:], func=ACT.Relu, scale=-1.0, bias=4.0)
            else:
                (nc.gpsimd if s in CLAMP_G else nc.vector).tensor_scalar(out=ee[s][:], in0=ee[s][:], scalar1=4.0, scalar2=1.0, op0=ALU.min, op1=ALU.add)

        def b_w(s):
            h, i = hi(s)
            osl = o_sb[i // 2][:, i % 2, NT * h:NT * (h + 1)]
            ww[s] = work.tile([P, NT], F32, name="ww", bufs=4)
            if s in CLAMP_S:
                nc.vector.scalar_tensor_tensor(out=ww[s][:], in0=ee[s][:], scalar=5.0, in1=osl, op0=ALU.subtract, op1=ALU.mult)
            elif s in W_G:
                for q in range(GSPLIT):
                    c = slice(NT // GSPLIT * q, NT // GSPLIT * (q + 1))
                    nc.gpsimd.tensor_tensor(out=ww[s][:, c], in0=ee[s][:, c], in1=osl[:, c], op=ALU.mult)
            else:
                nc.vector.tensor_tensor(out=ww[s][:], in0=ee[s][:], in1=osl, op=ALU.mult)

        def b_f(s):
            ff[s] = work.tile([P, NT], F32, name="ff")
            if s in CLAMP_S:
                nc.vector.tensor_tensor(out=ff[s][:], in0=z[s, 2][:], in1=er[s][:], op=ALU.subtract)
            else:
                nc.vector.tensor_tensor(out=ff[s][:], in0=er[s][:], in1=z[s, 2][:], op=ALU.subtract)

        def b_wf(s):
            nc.vector.tensor_tensor(out=ff[s][:], in0=ww[s][:], in1=ff[s][:], op=ALU.mult)

        def b_out(s):
            h, i = hi(s)
            ot = work.tile([P, NT], F32, name="ot", bufs=4)
            nc.vector.tensor_tensor(out=ot[:], in0=z[s, 2][:], in1=ff[s][:], op=ALU.add)
            nc.sync.dma_start(out=out[P * i:P * (i + 1), NT * h:NT * (h + 1)], in_=ot[:])

        calls = {
            "wid": wh_widen, "il": wh_inter, "q": wh_quant, "wil": w_inter, "wq": w_quant, "X": x_trans, "Xc": x_copy, "Xq": x_quant,
            "H": h_matmul, "Ht": h_tanh, "G": h_gain, "Q": h_quant, "t": b_tanh, "e": b_exp, "u": b_u, "sq": b_sq,
            "r": b_clamp, "f": b_f, "w": b_w, "wf": b_wf, "o": b_out,
            "z0": lambda s: z_matmul(s, 0), "z1": lambda s: z_matmul(s, 1), "z2": lambda s: z_matmul(s, 2),
        }
        HEAD = [("wid", 1, 0, 1), ("wid", 1, 0, 0), ("wid", 0, 0, 2), ("X", 1), ("X", 0), ("wid", 0, 0, 0), ("wid", 1, 0, 3), ("wid", 0, 0, 3), ("wid", 1, 0, 2), ("il", 1, 0), ("Xc", 1), ("wid", 0, 0, 1), ("wil", 0), ("Xc", 0), ("wid", 2, 0, 2), ("il", 0, 0), ("wil", 1), ("wid", 1, 1, 3), ("wq", 0), ("wid", 0, 1, 0), ("wq", 1), ("Xq", 1), ("wid", 1, 1, 0), ("Xq", 0), ("wid", 2, 0, 1), ("wid", 1, 1, 1), ("wid", 2, 0, 3), ("wid", 2, 1, 0), ("q", 0, 0), ("H", 1), ("wid", 0, 1, 2), ("wid", 2, 1, 2), ("H", 0), ("wid", 2, 1, 3), ("wid", 2, 1, 1), ("wid", 2, 0, 0), ("wid", 0, 1, 1), ("il", 2, 1), ("Ht", 0), ("wid", 1, 1, 2), ("wid", 0, 1, 3), ("Ht", 1), ("X", 3), ("X", 2), ("q", 1, 0), ("G", 0), ("il", 1, 1), ("Q", 0), ("il", 2, 0), ("q", 1, 1), ("q", 2, 0), ("q", 2, 1), ("il", 0, 1), ("z0", 0), ("Xc", 3), ("Xc", 2), ("z1", 0), ("q", 0, 1), ("Xq", 2), ("Xq", 3)]
        SLOT = [("z2", 0, 1), ("Xq", 4, 0), ("G", 2, 0), ("w", 0, 0), ("w", 0, 1), ("t", 1, 0), ("f", 0, 0), ("f", 0, 1), ("e", 1, 0), ("X", 5, 0), ("z2", 1, 0), ("wf", 0, 0), ("z1", 1, 1), ("r", 1, 0), ("Xc", 5, 0), ("u", 1, 0), ("z0", 1, 1), ("Q", 2, 0), ("wf", 0, 1), ("t", 1, 1), ("H", 3, 0), ("sq", 1, 0), ("u", 1, 1), ("o", 0, 0), ("e", 1, 1), ("z1", 2, 0), ("Ht", 3, 0), ("o", 0, 1), ("sq", 1, 1), ("r", 1, 1), ("z0", 2, 0)]
        done = set()
        for task in HEAD:
            calls[task[0]](*task[1:])
            done.add(task)
        for i in range(-1, NB + 1):
            for k, d, h in SLOT:
                task = (k, 2 * (i + d) + h) if k in BLOCKK else (k, i + d)
                if 0 <= i + d < NB and task not in done:
                    calls[k](*task[1:])
                    done.add(task)
